import numpy as np
import ml_dtypes


def mxq(x, axis, fmt="e4m3"):
    dtype, down = {"e4m3": (ml_dtypes.float8_e4m3fn, 7), "e5m2": (ml_dtypes.float8_e5m2, 14)}[fmt]
    v = np.moveaxis(np.asarray(x, np.float32).astype(ml_dtypes.bfloat16).astype(np.float64), axis, -1)
    blocks = v.reshape(v.shape[:-1] + (-1, 32))
    amax = np.abs(blocks).max(-1, keepdims=True)
    byte = np.maximum(np.where(amax > 0, np.frexp(amax)[1] - 1 + 127, 0) - down, 1)
    scale = np.exp2(byte - 127.0)
    codes = (blocks / scale).astype(np.float32).astype(dtype).astype(np.float64)
    return np.moveaxis((codes * scale).reshape(v.shape), -1, axis)


WIDE = False


def mx_kscale(k):
    if not WIDE:
        return np.ones(k)
    levels = np.array([10, -10, 5, -5, 0])
    if k % 512:
        return np.exp2(np.random.permutation(np.resize(levels, k // 32))).repeat(32)
    a = np.empty((k // 512, 16))
    for p in range(k // 512):
        a[p, :8] = np.random.permutation(np.resize(levels, 8))
        for g in range(8):
            far = levels[np.abs(levels - a[p, g]) >= 10]
            a[p, g + 8] = far[np.random.randint(len(far))]
    return np.exp2(a.ravel()).repeat(32)


def f64(x):
    return np.asarray(x).astype(np.float64)


def striped8(idx):
    return np.asarray(idx).reshape(8, -1, 16).transpose(0, 2, 1).reshape(128, -1).astype(np.uint16)


def unstriped8(offs):
    return offs.reshape(8, 16, -1).transpose(0, 2, 1).reshape(8, -1).astype(np.int64)


def pick8(x, idx, run):
    r = np.arange(len(x))
    return x[r[:, None], idx[r % (8 * run) // run]]


E2M1 = np.array([0.0, 0.5, 1.0, 1.5, 2.0, 3.0, 4.0, 6.0, -0.0, -0.5, -1.0, -1.5, -2.0, -3.0, -4.0, -6.0])


def pack_weight(w, fmt):
    k, n = w.shape
    w = f64(np.asarray(w, np.float32).astype(ml_dtypes.bfloat16)).reshape(k // 32, 32, n)
    amax = np.abs(w).max(1)
    if fmt == "e4m3":
        byte = np.frexp(amax)[1] - 1 + 127 - 7
    else:
        mant, ex = np.frexp(amax / 6.0)
        byte = np.where(mant > 0.5, ex, ex - 1) + 127
    byte = np.clip(np.where(amax > 0, byte, 1), 1, 254)
    scaled = (w * np.exp2(127.0 - byte)[:, None, :]).reshape(k, n).astype(np.float32)
    by_word = np.ascontiguousarray(scaled.reshape(k // 512, 128, 4, n).transpose(0, 1, 3, 2))
    if fmt == "e4m3":
        words = by_word.astype(ml_dtypes.float8_e4m3fn).view(np.uint8)
    else:
        c = by_word.astype(ml_dtypes.float4_e2m1fn).view(np.uint8) & 0xF
        words = (c[..., 0::2] | (c[..., 1::2] << 4)).reshape(k // 512, 128, 2 * n)
    return np.ascontiguousarray(words), np.ascontiguousarray(byte.astype(np.uint8).reshape(k // 512, 16, n))


def unpack_weight(words, scales, fmt):
    g, _, n = scales.shape
    words = np.ascontiguousarray(words).reshape(g, 128, n, -1)
    if fmt == "e4m3":
        vals = words.view(ml_dtypes.float8_e4m3fn).astype(np.float64)
    else:
        nib = np.empty((g, 128, n, 4), np.uint8)
        nib[..., 0::2] = words & 0xF
        nib[..., 1::2] = words >> 4
        vals = E2M1[nib]
    vals = vals * np.repeat(np.exp2(scales.astype(np.float64) - 127.0), 8, axis=1)[..., None]
    return vals.transpose(0, 1, 3, 2).reshape(g * 512, n)


D, K, T, U, X, I, J, M, Q = 512, 512, 1024, 1024, 1024, 512, 256, 128, 128


def setup_inputs():
    n = np.random.standard_normal
    idx = np.stack([np.random.permutation(U)[:I] for _ in range(8)])
    idx2 = np.stack([np.random.permutation(T)[:I] for _ in range(8)])
    idx3 = np.stack([np.random.permutation(T)[:J] for _ in range(8)])
    idx4 = np.stack([np.random.permutation(X)[:M] for _ in range(8)])
    idx5 = np.stack([np.random.permutation(U)[:M] for _ in range(8)])
    idx6 = np.stack([np.random.permutation(T)[:I] for _ in range(8)])
    idx7 = np.stack([np.random.permutation(X)[:I] for _ in range(8)])
    idx8 = np.stack([np.random.permutation(U)[:I] for _ in range(8)])
    fd = mx_kscale(D)
    fk = mx_kscale(K)
    wqp = pack_weight(n((D, K)) * 1.0 / np.sqrt(D) * fd[:, None] * fk, "e4m3")
    cachep = pack_weight(n((K, T)) * 1.0 / np.sqrt(K) / fk[:, None], "e4m3")
    draftp = pack_weight(n((K, U)) * 1.0 / np.sqrt(K) / fk[:, None], "e2m1")
    archp = pack_weight(n((D, X)) * 1.0 / np.sqrt(D) * fd[:, None], "e4m3")
    return {
        "states": (n((D, Q)) * 0.95 / fd[:, None]).astype(np.float32),
        "wq_words": wqp[0],
        "wq_scales": wqp[1],
        "cache_words": cachep[0],
        "cache_scales": cachep[1],
        "draft_words": draftp[0],
        "draft_scales": draftp[1],
        "arch_words": archp[0],
        "arch_scales": archp[1],
        "offs": striped8(idx),
        "offs2": striped8(idx2),
        "offs3": striped8(idx3),
        "offs4": striped8(idx4),
        "offs5": striped8(idx5),
        "offs6": striped8(idx6),
        "offs7": striped8(idx7),
        "offs8": striped8(idx8),
    }


def reference(states, wq_words, wq_scales, cache_words, cache_scales, draft_words, draft_scales, arch_words, arch_scales, offs, offs2, offs3, offs4, offs5, offs6, offs7, offs8):
    idx = unstriped8(offs)
    idx2 = unstriped8(offs2)
    idx3 = unstriped8(offs3)
    idx4 = unstriped8(offs4)
    idx5 = unstriped8(offs5)
    idx6 = unstriped8(offs6)
    idx7 = unstriped8(offs7)
    idx8 = unstriped8(offs8)
    wqu = unpack_weight(wq_words, wq_scales, "e4m3")
    cacheu = unpack_weight(cache_words, cache_scales, "e4m3")
    draftu = unpack_weight(draft_words, draft_scales, "e2m1")
    archu = unpack_weight(arch_words, arch_scales, "e4m3")
    statesq = mxq(f64(states), 0, "e4m3")
    qv = wqu.T @ statesq
    qvq = mxq(qv, 0, "e4m3")
    a = qvq.T @ cacheu
    b = qvq.T @ draftu
    c0 = statesq.T @ archu
    w = pick8(b, idx, 16) - pick8(a, idx2, 16)
    acc = w[:, 0:0 + J]
    rty = w[:, 256:256 + M]
    drp = w[:, 384:384 + M]
    f1 = np.zeros((Q, T))
    f1[np.arange(Q)[:, None], idx3[np.arange(Q) % 128 // 16]] = acc
    f2 = np.zeros((Q, X))
    f2[np.arange(Q)[:, None], idx4[np.arange(Q) % 128 // 16]] = rty
    f3 = np.zeros((Q, U))
    f3[np.arange(Q)[:, None], idx5[np.arange(Q) % 128 // 16]] = drp
    aa = a + f1
    cc = c0 - f2
    bb = b - f3
    v = np.maximum(pick8(aa, idx6, 16), pick8(cc, idx7, 16))
    y = v - pick8(bb, idx8, 16)
    return y

@@ -1,0 +1,228 @@
+from contextlib import ExitStack
+
+import concourse.mybir as mybir
+
+FLOPS = 469762048
+
+F32 = mybir.dt.float32
+BF16 = mybir.dt.bfloat16
+I32 = mybir.dt.int32
+U32 = mybir.dt.uint32
+U16 = mybir.dt.uint16
+U8 = mybir.dt.uint8
+FP8X4 = mybir.dt.float8_e4m3fn_x4
+FP4X4 = mybir.dt.float4_e2m1fn_x4
+COPY = mybir.ActivationFunctionType.Copy
+ADD = mybir.AluOpType.add
+SUB = mybir.AluOpType.subtract
+MAX = mybir.AluOpType.max
+
+P = 128
+PACK = 4
+K = 512
+Q = 128
+TOKENS = 1024
+BANK = 512
+SLOTS = 512
+HALF = 256
+RUN = 128
+
+
+def tile_attend_acceptretry_sidethree_kernel(
+    tc, states, wq_words, wq_scales, cache_words, cache_scales, draft_words, draft_scales,
+    arch_words, arch_scales, offs, offs2, offs3, offs4, offs5, offs6, offs7, offs8, out,
+):
+    nc = tc.nc
+    with ExitStack() as ctx:
+        lists = ctx.enter_context(tc.tile_pool(name="lists", bufs=1))
+        sb = ctx.enter_context(tc.tile_pool(name="sb", bufs=1))
+        psum = ctx.enter_context(tc.psum_pool(name="psum", bufs=1))
+
+        def scale_plane(name, width):
+            plane = sb.tile([P, width], U8, name=name, align_bytes=64)
+            nc.vector.memset(plane[:].bitcast(I32), 0)
+            return plane
+
+        def load_scales(name, scales, queue):
+            rows = sb.tile([4, 4, scales.shape[2] // 4], I32, name=name)
+            queue.dma_start(rows[:], scales[0].rearrange("(a r) n -> r a n", r=4).bitcast(I32))
+            return rows
+
+        def spread_scales(plane, rows, first_on_scalar):
+            if first_on_scalar:
+                nc.scalar.copy(plane[0:4, :].bitcast(U32), rows[:, 0, :].bitcast(U32))
+            else:
+                nc.vector.tensor_copy(plane[0:4, :].bitcast(I32), rows[:, 0, :])
+            for quad in range(1, 4):
+                nc.vector.tensor_copy(plane[32 * quad : 32 * quad + 4, :].bitcast(I32), rows[:, quad, :])
+
+        def load_words(name, words, first, width):
+            tile = sb.tile([P, width], U32, name=name, tag=name, align_bytes=64)
+            rows = words[0].rearrange("p n t -> p (n t)")
+            nc.sync.dma_start(tile[:].bitcast(I32), rows[:, PACK * first : PACK * (first + width)].bitcast(I32))
+            return tile
+
+        def load_list(name, src):
+            tile = lists.tile(list(src.shape), U16, name=name)
+            nc.sync.dma_start(tile[:], src)
+            return tile
+
+        wq_plane_raw = scale_plane("wq_plane_raw", K)
+        cache_plane = scale_plane("cache_plane", TOKENS)
+        draft_plane = scale_plane("draft_plane", TOKENS)
+        arch_plane = scale_plane("arch_plane", TOKENS)
+
+        states_raw = sb.tile([P, PACK, Q], F32, name="states_raw")
+        nc.sync.dma_start(states_raw[:], states.rearrange("(p j) q -> p j q", j=PACK))
+        wq_rows = load_scales("wq_rows", wq_scales, nc.scalar)
+        wq_raw = load_words("wq_raw", wq_words, 0, K)
+        cache_rows = load_scales("cache_rows", cache_scales, nc.scalar)
+        cache_codes = [load_words("cache_codes%d" % h, cache_words, BANK * h, BANK) for h in range(2)]
+        draft_rows = load_scales("draft_rows", draft_scales, nc.scalar)
+        draft_codes = sb.tile([P, 2 * TOKENS], U8, name="draft_codes", tag="draft_codes", align_bytes=64)
+        nc.sync.dma_start(draft_codes[:].bitcast(I32), draft_words[0].bitcast(I32))
+        arch_rows = load_scales("arch_rows", arch_scales, nc.sync)
+        arch_codes = load_words("arch_codes", arch_words, 0, TOKENS)
+        idx2 = load_list("idx2", offs2)
+        idx = load_list("idx", offs)
+        idx5 = load_list("idx5", offs5)
+        idx4 = load_list("idx4", offs4)
+        idx3 = load_list("idx3", offs3)
+        idx8 = load_list("idx8", offs8)
+        idx7 = load_list("idx7", offs7)
+        idx6 = load_list("idx6", offs6)
+
+        spread_scales(wq_plane_raw, wq_rows, False)
+
+        states_bf = sb.tile([P, Q, PACK], BF16, name="states_bf", align_bytes=64)
+        split = Q // 2
+        nc.scalar.activation(
+            states_bf[:, split:, :].rearrange("p (c i) t -> p c t i", i=4),
+            states_raw[:, :, split:].rearrange("p t (c i) -> p c t i", i=4),
+            COPY,
+        )
+        nc.vector.tensor_copy(
+            states_bf[:, :split, :].rearrange("p (c i) t -> p c t i", i=4),
+            states_raw[:, :, :split].rearrange("p t (c i) -> p c t i", i=4),
+        )
+        states_codes = sb.tile([P, Q], U32, name="states_codes", align_bytes=64)
+        states_plane = sb.tile([P, Q], U8, name="states_plane", align_bytes=64)
+        nc.vector.quantize_mx(
+            states_codes[:].bitcast(FP8X4), states_plane[:], states_bf[:].rearrange("p q t -> p (q t)")
+        )
+
+        wq_codes = sb.tile([P, K], U32, name="wq_codes", align_bytes=64)
+        wq_plane = sb.tile([P, K], U8, name="wq_plane", align_bytes=64)
+        nc.vector.tensor_copy(
+            wq_plane[:].rearrange("p (t m) -> p m t", t=PACK),
+            wq_plane_raw[:].rearrange("p (m t) -> p m t", t=PACK),
+        )
+        nc.scalar.copy(
+            wq_codes[:].rearrange("p (t m) -> p m t", t=PACK),
+            wq_raw[:].rearrange("p (m t) -> p m t", t=PACK),
+        )
+
+        spread_scales(cache_plane, cache_rows, True)
+        spread_scales(draft_plane, draft_rows, True)
+        qv_ps = psum.tile([P, PACK, Q], F32, name="qv_ps")
+        for t in range(PACK):
+            cols = slice(P * t, P * (t + 1))
+            nc.tensor.matmul_mx(
+                qv_ps[:, t, :],
+                lhsT=wq_codes[:, cols].bitcast(FP8X4), lhsT_scale=wq_plane[:, cols],
+                rhs=states_codes[:].bitcast(FP8X4), rhs_scale=states_plane[:],
+                start=True, stop=True,
+            )
+        qv_bf = sb.tile([P, Q, PACK], BF16, name="qv_bf", tag="qv_bf", align_bytes=64)
+        nc.scalar.activation(qv_bf[:], qv_ps[:].rearrange("p t q -> p q t"), COPY)
+        qv_codes = sb.tile([P, Q], U32, name="qv_codes", align_bytes=64)
+        qv_plane = sb.tile([P, Q], U8, name="qv_plane", align_bytes=64)
+        nc.vector.quantize_mx(qv_codes[:].bitcast(FP8X4), qv_plane[:], qv_bf[:].rearrange("p q t -> p (q t)"))
+        spread_scales(arch_plane, arch_rows, True)
+
+        def score(name, codes, plane, moving, moving_plane):
+            bank = psum.tile([P, moving_plane.shape[1]], F32, name=name)
+            nc.tensor.matmul_mx(
+                bank[:], lhsT=codes[:].bitcast(FP8X4), lhsT_scale=plane[:],
+                rhs=moving, rhs_scale=moving_plane, start=True, stop=True,
+            )
+            return bank
+
+        a_ps = [
+            score("a_ps%d" % h, qv_codes, qv_plane, cache_codes[h][:].bitcast(FP8X4),
+                  cache_plane[:, BANK * h : BANK * (h + 1)])
+            for h in range(2)
+        ]
+        b_cuts = [(0, 512), (512, 768), (768, 1024)]
+        b_ps = [
+            score("b_ps%d" % lo, qv_codes, qv_plane, draft_codes[:, 2 * lo : 2 * hi].bitcast(FP4X4),
+                  draft_plane[:, lo:hi])
+            for lo, hi in b_cuts
+        ]
+        c_ps = [
+            score("c_ps%d" % h, states_codes, states_plane,
+                  arch_codes[:, BANK * h : BANK * (h + 1)].bitcast(FP8X4),
+                  arch_plane[:, BANK * h : BANK * (h + 1)])
+            for h in range(2)
+        ]
+
+        f3 = sb.tile([P, TOKENS], F32, name="f3", tag="cache_codes0", align_bytes=64)
+        f2 = sb.tile([P, TOKENS], F32, name="f2", tag="cache_codes1", align_bytes=64)
+        f1 = sb.tile([P, TOKENS], F32, name="f1", tag="draft_codes", align_bytes=64)
+        for window in (f3, f2, f1):
+            nc.gpsimd.memset(window[:], 0.0)
+
+        late = slice(HALF // 16, SLOTS // 16)
+        early = slice(0, HALF // 16)
+
+        a = sb.tile([P, TOKENS], F32, name="a")
+        b = sb.tile([P, TOKENS], F32, name="b")
+        nc.scalar.activation(a[:, :BANK], a_ps[0][:], COPY)
+        nc.vector.tensor_copy(a[:, BANK:], a_ps[1][:])
+        a_late = sb.tile([P, HALF], F32, name="a_late")
+        a_early = sb.tile([P, HALF], F32, name="a_early")
+        nc.scalar.activation(a_late[:], a[:].indirect(idx2[:, late]), COPY)
+        nc.vector.tensor_copy(b[:, 0:512], b_ps[0][:])
+        nc.vector.tensor_copy(b[:, 512:768], b_ps[1][:])
+        nc.scalar.activation(b[:, 768:1024], b_ps[2][:], COPY)
+        w_late = sb.tile([P, HALF], F32, name="w_late")
+        acc = sb.tile([P, HALF], F32, name="acc")
+        nc.vector.tensor_tensor(w_late[:], b[:].indirect(idx[:, late]), a_late[:], SUB)
+        nc.scalar.activation(a_early[:], a[:].indirect(idx2[:, early]), COPY)
+        nc.vector.tensor_tensor(acc[:], b[:].indirect(idx[:, early]), a_early[:], SUB)
+
+        nc.scalar.activation(f3[:].indirect(idx5[:]), w_late[:, RUN:], COPY)
+        nc.scalar.activation(f2[:].indirect(idx4[:]), w_late[:, :RUN], COPY)
+        nc.scalar.activation(f1[:].indirect(idx3[:]), acc[:], COPY)
+
+        bb = sb.tile([P, TOKENS], F32, name="bb")
+        cc = sb.tile([P, TOKENS], F32, name="cc")
+        aa = sb.tile([P, TOKENS], F32, name="aa")
+        nc.vector.tensor_tensor(bb[:], b[:], f3[:], SUB)
+        for h in range(2):
+            cols = slice(BANK * h, BANK * (h + 1))
+            nc.vector.tensor_tensor(cc[:, cols], c_ps[h][:], f2[:, cols], SUB)
+        nc.vector.tensor_tensor(aa[:], a[:], f1[:], ADD)
+
+        bb_early = sb.tile([P, HALF], F32, name="bb_early")
+        bb_late = sb.tile([P, HALF], F32, name="bb_late")
+        cc_late = sb.tile([P, HALF], F32, name="cc_late")
+        aa_late = sb.tile([P, HALF], F32, name="aa_late")
+        nc.scalar.activation(bb_early[:], bb[:].indirect(idx8[:, early]), COPY)
+        nc.scalar.activation(bb_late[:], bb[:].indirect(idx8[:, late]), COPY)
+        nc.scalar.activation(cc_late[:], cc[:].indirect(idx7[:, late]), COPY)
+        nc.scalar.activation(aa_late[:], aa[:].indirect(idx6[:, late]), COPY)
+
+        cc_less = sb.tile([P, HALF], F32, name="cc_less")
+        aa_less = sb.tile([P, HALF], F32, name="aa_less")
+        y_early = sb.tile([P, HALF], F32, name="y_early")
+        nc.vector.tensor_tensor(cc_less[:], cc[:].indirect(idx7[:, early]), bb_early[:], SUB)
+        nc.vector.tensor_tensor(aa_less[:], aa[:].indirect(idx6[:, early]), bb_early[:], SUB)
+        nc.vector.tensor_tensor(y_early[:], aa_less[:], cc_less[:], MAX)
+        nc.sync.dma_start(out[:, :HALF], y_early[:])
+
+        v_late = sb.tile([P, HALF], F32, name="v_late")
+        y_late = sb.tile([P, HALF], F32, name="y_late")
+        nc.vector.tensor_tensor(v_late[:], aa_late[:], cc_late[:], MAX)
+        nc.vector.tensor_tensor(y_late[:], v_late[:], bb_late[:], SUB)
+        nc.sync.dma_start(out[:, HALF:], y_late[:])

@@ -39,22 +39,16 @@ def tile_attend_acceptretry_sidethree_kernel(
         psum = ctx.enter_context(tc.psum_pool(name="psum", bufs=1))
 
         def scale_plane(name, width):
-            plane = sb.tile([P, width], U8, name=name, align_bytes=64)
+            plane = sb.tile([P, width], U8, name=name, tag=name, align_bytes=64)
             nc.vector.memset(plane[:].bitcast(I32), 0)
             return plane
 
-        def load_scales(name, scales, queue):
-            rows = sb.tile([4, 4, scales.shape[2] // 4], I32, name=name)
-            queue.dma_start(rows[:], scales[0].rearrange("(a r) n -> r a n", r=4).bitcast(I32))
-            return rows
-
-        def spread_scales(plane, rows, first_on_scalar):
-            if first_on_scalar:
-                nc.scalar.copy(plane[0:4, :].bitcast(U32), rows[:, 0, :].bitcast(U32))
-            else:
-                nc.vector.tensor_copy(plane[0:4, :].bitcast(I32), rows[:, 0, :])
-            for quad in range(1, 4):
-                nc.vector.tensor_copy(plane[32 * quad : 32 * quad + 4, :].bitcast(I32), rows[:, quad, :])
+        def load_scales(plane, scales):
+            for quad in range(4):
+                nc.sync.dma_start(
+                    plane[32 * quad : 32 * quad + 4, :].bitcast(I32),
+                    scales[0, 4 * quad : 4 * quad + 4, :].bitcast(I32),
+                )
 
         def load_words(name, words, first, width):
             tile = sb.tile([P, width], U32, name=name, tag=name, align_bytes=64)
@@ -74,25 +68,26 @@ def tile_attend_acceptretry_sidethree_kernel(
 
         states_raw = sb.tile([P, PACK, Q], F32, name="states_raw")
         nc.sync.dma_start(states_raw[:], states.rearrange("(p j) q -> p j q", j=PACK))
-        wq_rows = load_scales("wq_rows", wq_scales, nc.scalar)
         wq_raw = load_words("wq_raw", wq_words, 0, K)
-        cache_rows = load_scales("cache_rows", cache_scales, nc.scalar)
-        cache_codes = [load_words("cache_codes%d" % h, cache_words, BANK * h, BANK) for h in range(2)]
-        draft_rows = load_scales("draft_rows", draft_scales, nc.scalar)
-        draft_codes = sb.tile([P, 2 * TOKENS], U8, name="draft_codes", tag="draft_codes", align_bytes=64)
+        load_scales(wq_plane_raw, wq_scales)
+        cache_codes = load_words("cache_codes", cache_words, 0, TOKENS)
+        load_scales(cache_plane, cache_scales)
+        draft_codes = sb.tile([P, 2 * TOKENS], U8, name="draft_codes", align_bytes=64)
         nc.sync.dma_start(draft_codes[:].bitcast(I32), draft_words[0].bitcast(I32))
-        arch_rows = load_scales("arch_rows", arch_scales, nc.sync)
-        arch_codes = load_words("arch_codes", arch_words, 0, TOKENS)
+        load_scales(draft_plane, draft_scales)
         idx2 = load_list("idx2", offs2)
         idx = load_list("idx", offs)
+        arch_codes = load_words("arch_codes", arch_words, 0, TOKENS)
         idx5 = load_list("idx5", offs5)
         idx4 = load_list("idx4", offs4)
         idx3 = load_list("idx3", offs3)
+        load_scales(arch_plane, arch_scales)
         idx8 = load_list("idx8", offs8)
         idx7 = load_list("idx7", offs7)
         idx6 = load_list("idx6", offs6)
 
-        spread_scales(wq_plane_raw, wq_rows, False)
+        f3 = sb.tile([P, TOKENS], F32, name="f3")
+        nc.vector.memset(f3[:], 0.0)
 
         states_bf = sb.tile([P, Q, PACK], BF16, name="states_bf", align_bytes=64)
         split = Q // 2
@@ -114,16 +109,16 @@ def tile_attend_acceptretry_sidethree_kernel(
         wq_codes = sb.tile([P, K], U32, name="wq_codes", align_bytes=64)
         wq_plane = sb.tile([P, K], U8, name="wq_plane", align_bytes=64)
         nc.vector.tensor_copy(
-            wq_plane[:].rearrange("p (t m) -> p m t", t=PACK),
-            wq_plane_raw[:].rearrange("p (m t) -> p m t", t=PACK),
+            wq_plane[:].rearrange("p (t m) -> p t m", t=PACK),
+            wq_plane_raw[:].rearrange("p (m t) -> p t m", t=PACK),
         )
         nc.scalar.copy(
-            wq_codes[:].rearrange("p (t m) -> p m t", t=PACK),
-            wq_raw[:].rearrange("p (m t) -> p m t", t=PACK),
+            wq_codes[:].rearrange("p (t c i) -> p c t i", t=PACK, i=4),
+            wq_raw[:].rearrange("p (c i t) -> p c t i", t=PACK, i=4),
         )
 
-        spread_scales(cache_plane, cache_rows, True)
-        spread_scales(draft_plane, draft_rows, True)
+        f2 = sb.tile([P, TOKENS], F32, name="f2", tag="wq_plane_raw", align_bytes=64)
+        nc.vector.memset(f2[:], 0.0)
         qv_ps = psum.tile([P, PACK, Q], F32, name="qv_ps")
         for t in range(PACK):
             cols = slice(P * t, P * (t + 1))
@@ -138,7 +133,8 @@ def tile_attend_acceptretry_sidethree_kernel(
         qv_codes = sb.tile([P, Q], U32, name="qv_codes", align_bytes=64)
         qv_plane = sb.tile([P, Q], U8, name="qv_plane", align_bytes=64)
         nc.vector.quantize_mx(qv_codes[:].bitcast(FP8X4), qv_plane[:], qv_bf[:].rearrange("p q t -> p (q t)"))
-        spread_scales(arch_plane, arch_rows, True)
+        f1 = sb.tile([P, TOKENS], F32, name="f1", tag="qv_bf", align_bytes=64)
+        nc.vector.memset(f1[:], 0.0)
 
         def score(name, codes, plane, moving, moving_plane):
             bank = psum.tile([P, moving_plane.shape[1]], F32, name=name)
@@ -149,7 +145,7 @@ def tile_attend_acceptretry_sidethree_kernel(
             return bank
 
         a_ps = [
-            score("a_ps%d" % h, qv_codes, qv_plane, cache_codes[h][:].bitcast(FP8X4),
+            score("a_ps%d" % h, qv_codes, qv_plane, cache_codes[:, BANK * h : BANK * (h + 1)].bitcast(FP8X4),
                   cache_plane[:, BANK * h : BANK * (h + 1)])
             for h in range(2)
         ]
@@ -165,12 +161,6 @@ def tile_attend_acceptretry_sidethree_kernel(
                   arch_plane[:, BANK * h : BANK * (h + 1)])
             for h in range(2)
         ]
-
-        f3 = sb.tile([P, TOKENS], F32, name="f3", tag="cache_codes0", align_bytes=64)
-        f2 = sb.tile([P, TOKENS], F32, name="f2", tag="cache_codes1", align_bytes=64)
-        f1 = sb.tile([P, TOKENS], F32, name="f1", tag="draft_codes", align_bytes=64)
-        for window in (f3, f2, f1):
-            nc.gpsimd.memset(window[:], 0.0)
 
         late = slice(HALF // 16, SLOTS // 16)
         early = slice(0, HALF // 16)
@@ -197,11 +187,11 @@ def tile_attend_acceptretry_sidethree_kernel(
 
         bb = sb.tile([P, TOKENS], F32, name="bb")
         cc = sb.tile([P, TOKENS], F32, name="cc")
-        aa = sb.tile([P, TOKENS], F32, name="aa")
         nc.vector.tensor_tensor(bb[:], b[:], f3[:], SUB)
         for h in range(2):
             cols = slice(BANK * h, BANK * (h + 1))
             nc.vector.tensor_tensor(cc[:, cols], c_ps[h][:], f2[:, cols], SUB)
+        aa = sb.tile([P, TOKENS], F32, name="aa", tag="wq_plane_raw", align_bytes=64)
         nc.vector.tensor_tensor(aa[:], a[:], f1[:], ADD)
 
         bb_early = sb.tile([P, HALF], F32, name="bb_early")

@@ -38,9 +38,9 @@ def tile_attend_acceptretry_sidethree_kernel(
         sb = ctx.enter_context(tc.tile_pool(name="sb", bufs=1))
         psum = ctx.enter_context(tc.psum_pool(name="psum", bufs=1))
 
-        def scale_plane(name, width):
+        def scale_plane(name, width, engine=nc.vector):
             plane = sb.tile([P, width], U8, name=name, tag=name, align_bytes=64)
-            nc.vector.memset(plane[:].bitcast(I32), 0)
+            engine.memset(plane[:].bitcast(I32), 0)
             return plane
 
         def load_scales(plane, scales):
@@ -61,27 +61,27 @@ def tile_attend_acceptretry_sidethree_kernel(
             nc.sync.dma_start(tile[:], src)
             return tile
 
-        wq_plane_raw = scale_plane("wq_plane_raw", K)
+        wq_plane_raw = scale_plane("wq_plane_raw", K, nc.gpsimd)
         cache_plane = scale_plane("cache_plane", TOKENS)
         draft_plane = scale_plane("draft_plane", TOKENS)
         arch_plane = scale_plane("arch_plane", TOKENS)
 
         states_raw = sb.tile([P, PACK, Q], F32, name="states_raw")
         nc.sync.dma_start(states_raw[:], states.rearrange("(p j) q -> p j q", j=PACK))
-        wq_raw = load_words("wq_raw", wq_words, 0, K)
         load_scales(wq_plane_raw, wq_scales)
+        wq_raw = load_words("wq_raw", wq_words, 0, K)
         cache_codes = load_words("cache_codes", cache_words, 0, TOKENS)
-        load_scales(cache_plane, cache_scales)
         draft_codes = sb.tile([P, 2 * TOKENS], U8, name="draft_codes", align_bytes=64)
         nc.sync.dma_start(draft_codes[:].bitcast(I32), draft_words[0].bitcast(I32))
+        load_scales(cache_plane, cache_scales)
         load_scales(draft_plane, draft_scales)
         idx2 = load_list("idx2", offs2)
         idx = load_list("idx", offs)
-        arch_codes = load_words("arch_codes", arch_words, 0, TOKENS)
         idx5 = load_list("idx5", offs5)
         idx4 = load_list("idx4", offs4)
-        idx3 = load_list("idx3", offs3)
+        arch_codes = load_words("arch_codes", arch_words, 0, TOKENS)
         load_scales(arch_plane, arch_scales)
+        idx3 = load_list("idx3", offs3)
         idx8 = load_list("idx8", offs8)
         idx7 = load_list("idx7", offs7)
         idx6 = load_list("idx6", offs6)
@@ -106,25 +106,31 @@ def tile_attend_acceptretry_sidethree_kernel(
             states_codes[:].bitcast(FP8X4), states_plane[:], states_bf[:].rearrange("p q t -> p (q t)")
         )
 
-        wq_codes = sb.tile([P, K], U32, name="wq_codes", align_bytes=64)
         wq_plane = sb.tile([P, K], U8, name="wq_plane", align_bytes=64)
         nc.vector.tensor_copy(
             wq_plane[:].rearrange("p (t m) -> p t m", t=PACK),
             wq_plane_raw[:].rearrange("p (m t) -> p t m", t=PACK),
         )
-        nc.scalar.copy(
-            wq_codes[:].rearrange("p (t c i) -> p c t i", t=PACK, i=4),
-            wq_raw[:].rearrange("p (c i t) -> p c t i", t=PACK, i=4),
-        )
+        wq_by_place = wq_raw[:].rearrange("p (c i t) -> p c t i", t=PACK, i=4)
+        wq_codes = []
+        for first, count in ((0, 2), (2, 1), (3, 1)):
+            part = sb.tile([P, count, P], U32, name="wq_codes%d" % first, align_bytes=64)
+            dst = part[:].rearrange("p t (c i) -> p c t i", i=4)
+            src = wq_by_place[:, :, first : first + count, :]
+            if first < 3:
+                nc.scalar.copy(dst, src)
+            else:
+                nc.vector.tensor_copy(dst.bitcast(I32), src.bitcast(I32))
+            wq_codes.extend(part[:, t, :] for t in range(count))
 
-        f2 = sb.tile([P, TOKENS], F32, name="f2", tag="wq_plane_raw", align_bytes=64)
+        f2 = sb.tile([P, TOKENS], F32, name="f2", tag="wq_raw", align_bytes=64)
         nc.vector.memset(f2[:], 0.0)
-        qv_ps = psum.tile([P, PACK, Q], F32, name="qv_ps")
+        qv_ps = psum.tile([P, PACK, Q], F32, name="qv_ps", tag="c_ps0")
         for t in range(PACK):
             cols = slice(P * t, P * (t + 1))
             nc.tensor.matmul_mx(
                 qv_ps[:, t, :],
-                lhsT=wq_codes[:, cols].bitcast(FP8X4), lhsT_scale=wq_plane[:, cols],
+                lhsT=wq_codes[t].bitcast(FP8X4), lhsT_scale=wq_plane[:, cols],
                 rhs=states_codes[:].bitcast(FP8X4), rhs_scale=states_plane[:],
                 start=True, stop=True,
             )
@@ -137,19 +143,18 @@ def tile_attend_acceptretry_sidethree_kernel(
         nc.vector.memset(f1[:], 0.0)
 
         def score(name, codes, plane, moving, moving_plane):
-            bank = psum.tile([P, moving_plane.shape[1]], F32, name=name)
+            bank = psum.tile([P, moving_plane.shape[1]], F32, name=name, tag=name)
             nc.tensor.matmul_mx(
                 bank[:], lhsT=codes[:].bitcast(FP8X4), lhsT_scale=plane[:],
                 rhs=moving, rhs_scale=moving_plane, start=True, stop=True,
             )
             return bank
 
-        a_ps = [
-            score("a_ps%d" % h, qv_codes, qv_plane, cache_codes[:, BANK * h : BANK * (h + 1)].bitcast(FP8X4),
-                  cache_plane[:, BANK * h : BANK * (h + 1)])
-            for h in range(2)
-        ]
         b_cuts = [(0, 512), (512, 768), (768, 1024)]
+        a_ps = [
+            score("a_ps%d" % lo, qv_codes, qv_plane, cache_codes[:, lo:hi].bitcast(FP8X4), cache_plane[:, lo:hi])
+            for lo, hi in b_cuts
+        ]
         b_ps = [
             score("b_ps%d" % lo, qv_codes, qv_plane, draft_codes[:, 2 * lo : 2 * hi].bitcast(FP4X4),
                   draft_plane[:, lo:hi])
@@ -168,7 +173,8 @@ def tile_attend_acceptretry_sidethree_kernel(
         a = sb.tile([P, TOKENS], F32, name="a")
         b = sb.tile([P, TOKENS], F32, name="b")
         nc.scalar.activation(a[:, :BANK], a_ps[0][:], COPY)
-        nc.vector.tensor_copy(a[:, BANK:], a_ps[1][:])
+        nc.vector.tensor_copy(a[:, 512:768], a_ps[1][:])
+        nc.vector.tensor_copy(a[:, 768:1024], a_ps[2][:])
         a_late = sb.tile([P, HALF], F32, name="a_late")
         a_early = sb.tile([P, HALF], F32, name="a_early")
         nc.scalar.activation(a_late[:], a[:].indirect(idx2[:, late]), COPY)
@@ -187,32 +193,37 @@ def tile_attend_acceptretry_sidethree_kernel(
 
         bb = sb.tile([P, TOKENS], F32, name="bb")
         cc = sb.tile([P, TOKENS], F32, name="cc")
-        nc.vector.tensor_tensor(bb[:], b[:], f3[:], SUB)
+        nc.gpsimd.tensor_tensor(bb[:, 768:], b[:, 768:], f3[:, 768:], SUB)
+        for bank, (lo, hi) in zip(b_ps, b_cuts[:2]):
+            nc.vector.tensor_tensor(bb[:, lo:hi], bank[:], f3[:, lo:hi], SUB)
         for h in range(2):
             cols = slice(BANK * h, BANK * (h + 1))
             nc.vector.tensor_tensor(cc[:, cols], c_ps[h][:], f2[:, cols], SUB)
-        aa = sb.tile([P, TOKENS], F32, name="aa", tag="wq_plane_raw", align_bytes=64)
-        nc.vector.tensor_tensor(aa[:], a[:], f1[:], ADD)
-
         bb_early = sb.tile([P, HALF], F32, name="bb_early")
-        bb_late = sb.tile([P, HALF], F32, name="bb_late")
+        nc.vector.tensor_copy(bb_early[:], bb[:].indirect(idx8[:, early]))
+        aa = sb.tile([P, TOKENS], F32, name="aa", tag="wq_raw", align_bytes=64)
+        nc.gpsimd.tensor_tensor(aa[:, 768:], a[:, 768:], f1[:, 768:], ADD)
+        for bank, (lo, hi) in zip(a_ps, b_cuts[:2]):
+            nc.vector.tensor_tensor(aa[:, lo:hi], bank[:], f1[:, lo:hi], ADD)
+
+        cc_early = sb.tile([P, HALF], F32, name="cc_early")
         cc_late = sb.tile([P, HALF], F32, name="cc_late")
         aa_late = sb.tile([P, HALF], F32, name="aa_late")
-        nc.scalar.activation(bb_early[:], bb[:].indirect(idx8[:, early]), COPY)
-        nc.scalar.activation(bb_late[:], bb[:].indirect(idx8[:, late]), COPY)
+        bb_late = sb.tile([P, HALF], F32, name="bb_late", tag="qv_bf", align_bytes=64)
+        nc.scalar.activation(cc_early[:], cc[:].indirect(idx7[:, early]), COPY)
         nc.scalar.activation(cc_late[:], cc[:].indirect(idx7[:, late]), COPY)
         nc.scalar.activation(aa_late[:], aa[:].indirect(idx6[:, late]), COPY)
+        nc.scalar.activation(bb_late[:], bb[:].indirect(idx8[:, late]), COPY)
 
         cc_less = sb.tile([P, HALF], F32, name="cc_less")
         aa_less = sb.tile([P, HALF], F32, name="aa_less")
+        v_late = sb.tile([P, HALF], F32, name="v_late")
         y_early = sb.tile([P, HALF], F32, name="y_early")
-        nc.vector.tensor_tensor(cc_less[:], cc[:].indirect(idx7[:, early]), bb_early[:], SUB)
+        y_late = sb.tile([P, HALF], F32, name="y_late")
+        nc.vector.tensor_tensor(cc_less[:], cc_early[:], bb_early[:], SUB)
         nc.vector.tensor_tensor(aa_less[:], aa[:].indirect(idx6[:, early]), bb_early[:], SUB)
+        nc.vector.tensor_tensor(v_late[:], aa_late[:], cc_late[:], MAX)
         nc.vector.tensor_tensor(y_early[:], aa_less[:], cc_less[:], MAX)
         nc.sync.dma_start(out[:, :HALF], y_early[:])
-
-        v_late = sb.tile([P, HALF], F32, name="v_late")
-        y_late = sb.tile([P, HALF], F32, name="y_late")
-        nc.vector.tensor_tensor(v_late[:], aa_late[:], cc_late[:], MAX)
         nc.vector.tensor_tensor(y_late[:], v_late[:], bb_late[:], SUB)
         nc.sync.dma_start(out[:, HALF:], y_late[:])

@@ -62,25 +62,25 @@ def tile_attend_acceptretry_sidethree_kernel(
             return tile
 
         wq_plane_raw = scale_plane("wq_plane_raw", K, nc.gpsimd)
+        arch_plane = scale_plane("arch_plane", TOKENS)
         cache_plane = scale_plane("cache_plane", TOKENS)
         draft_plane = scale_plane("draft_plane", TOKENS)
-        arch_plane = scale_plane("arch_plane", TOKENS)
 
         states_raw = sb.tile([P, PACK, Q], F32, name="states_raw")
         nc.sync.dma_start(states_raw[:], states.rearrange("(p j) q -> p j q", j=PACK))
         load_scales(wq_plane_raw, wq_scales)
         wq_raw = load_words("wq_raw", wq_words, 0, K)
+        arch_codes = load_words("arch_codes", arch_words, 0, TOKENS)
+        load_scales(arch_plane, arch_scales)
         cache_codes = load_words("cache_codes", cache_words, 0, TOKENS)
+        load_scales(cache_plane, cache_scales)
         draft_codes = sb.tile([P, 2 * TOKENS], U8, name="draft_codes", align_bytes=64)
         nc.sync.dma_start(draft_codes[:].bitcast(I32), draft_words[0].bitcast(I32))
-        load_scales(cache_plane, cache_scales)
         load_scales(draft_plane, draft_scales)
         idx2 = load_list("idx2", offs2)
         idx = load_list("idx", offs)
         idx5 = load_list("idx5", offs5)
         idx4 = load_list("idx4", offs4)
-        arch_codes = load_words("arch_codes", arch_words, 0, TOKENS)
-        load_scales(arch_plane, arch_scales)
         idx3 = load_list("idx3", offs3)
         idx8 = load_list("idx8", offs8)
         idx7 = load_list("idx7", offs7)
@@ -125,7 +125,7 @@ def tile_attend_acceptretry_sidethree_kernel(
 
         f2 = sb.tile([P, TOKENS], F32, name="f2", tag="wq_raw", align_bytes=64)
         nc.vector.memset(f2[:], 0.0)
-        qv_ps = psum.tile([P, PACK, Q], F32, name="qv_ps", tag="c_ps0")
+        qv_ps = psum.tile([P, PACK, Q], F32, name="qv_ps", tag="b_ps768")
         for t in range(PACK):
             cols = slice(P * t, P * (t + 1))
             nc.tensor.matmul_mx(
@@ -134,14 +134,6 @@ def tile_attend_acceptretry_sidethree_kernel(
                 rhs=states_codes[:].bitcast(FP8X4), rhs_scale=states_plane[:],
                 start=True, stop=True,
             )
-        qv_bf = sb.tile([P, Q, PACK], BF16, name="qv_bf", tag="qv_bf", align_bytes=64)
-        nc.scalar.activation(qv_bf[:], qv_ps[:].rearrange("p t q -> p q t"), COPY)
-        qv_codes = sb.tile([P, Q], U32, name="qv_codes", align_bytes=64)
-        qv_plane = sb.tile([P, Q], U8, name="qv_plane", align_bytes=64)
-        nc.vector.quantize_mx(qv_codes[:].bitcast(FP8X4), qv_plane[:], qv_bf[:].rearrange("p q t -> p (q t)"))
-        f1 = sb.tile([P, TOKENS], F32, name="f1", tag="qv_bf", align_bytes=64)
-        nc.vector.memset(f1[:], 0.0)
-
         def score(name, codes, plane, moving, moving_plane):
             bank = psum.tile([P, moving_plane.shape[1]], F32, name=name, tag=name)
             nc.tensor.matmul_mx(
@@ -149,6 +141,21 @@ def tile_attend_acceptretry_sidethree_kernel(
                 rhs=moving, rhs_scale=moving_plane, start=True, stop=True,
             )
             return bank
+
+        c_ps = [
+            score("c_ps%d" % h, states_codes, states_plane,
+                  arch_codes[:, BANK * h : BANK * (h + 1)].bitcast(FP8X4),
+                  arch_plane[:, BANK * h : BANK * (h + 1)])
+            for h in range(2)
+        ]
+
+        qv_bf = sb.tile([P, Q, PACK], BF16, name="qv_bf", tag="qv_bf", align_bytes=64)
+        nc.scalar.activation(qv_bf[:], qv_ps[:].rearrange("p t q -> p q t"), COPY)
+        qv_codes = sb.tile([P, Q], U32, name="qv_codes", align_bytes=64)
+        qv_plane = sb.tile([P, Q], U8, name="qv_plane", align_bytes=64)
+        nc.vector.quantize_mx(qv_codes[:].bitcast(FP8X4), qv_plane[:], qv_bf[:].rearrange("p q t -> p (q t)"))
+        f1 = sb.tile([P, TOKENS], F32, name="f1", tag="qv_bf", align_bytes=64)
+        nc.vector.memset(f1[:], 0.0)
 
         b_cuts = [(0, 512), (512, 768), (768, 1024)]
         a_ps = [
@@ -159,12 +166,6 @@ def tile_attend_acceptretry_sidethree_kernel(
             score("b_ps%d" % lo, qv_codes, qv_plane, draft_codes[:, 2 * lo : 2 * hi].bitcast(FP4X4),
                   draft_plane[:, lo:hi])
             for lo, hi in b_cuts
-        ]
-        c_ps = [
-            score("c_ps%d" % h, states_codes, states_plane,
-                  arch_codes[:, BANK * h : BANK * (h + 1)].bitcast(FP8X4),
-                  arch_plane[:, BANK * h : BANK * (h + 1)])
-            for h in range(2)
         ]
 
         late = slice(HALF // 16, SLOTS // 16)

from contextlib import ExitStack

import concourse.mybir as mybir

FLOPS = 469762048

F32 = mybir.dt.float32
BF16 = mybir.dt.bfloat16
I32 = mybir.dt.int32
U32 = mybir.dt.uint32
U16 = mybir.dt.uint16
U8 = mybir.dt.uint8
FP8X4 = mybir.dt.float8_e4m3fn_x4
FP4X4 = mybir.dt.float4_e2m1fn_x4
COPY = mybir.ActivationFunctionType.Copy
ADD = mybir.AluOpType.add
SUB = mybir.AluOpType.subtract
MAX = mybir.AluOpType.max

P = 128
PACK = 4
K = 512
Q = 128
TOKENS = 1024
BANK = 512
SLOTS = 512
HALF = 256
RUN = 128


def tile_attend_acceptretry_sidethree_kernel(
    tc, states, wq_words, wq_scales, cache_words, cache_scales, draft_words, draft_scales,
    arch_words, arch_scales, offs, offs2, offs3, offs4, offs5, offs6, offs7, offs8, out,
):
    nc = tc.nc
    with ExitStack() as ctx:
        lists = ctx.enter_context(tc.tile_pool(name="lists", bufs=1))
        sb = ctx.enter_context(tc.tile_pool(name="sb", bufs=1))
        psum = ctx.enter_context(tc.psum_pool(name="psum", bufs=1))

        def scale_plane(name, width, engine=nc.vector):
            plane = sb.tile([P, width], U8, name=name, tag=name, align_bytes=64)
            engine.memset(plane[:].bitcast(I32), 0)
            return plane

        def load_scales(plane, scales):
            for quad in range(4):
                nc.sync.dma_start(
                    plane[32 * quad : 32 * quad + 4, :].bitcast(I32),
                    scales[0, 4 * quad : 4 * quad + 4, :].bitcast(I32),
                )

        def load_words(name, words, first, width):
            tile = sb.tile([P, width], U32, name=name, tag=name, align_bytes=64)
            rows = words[0].rearrange("p n t -> p (n t)")
            nc.sync.dma_start(tile[:].bitcast(I32), rows[:, PACK * first : PACK * (first + width)].bitcast(I32))
            return tile

        def load_list(name, src):
            tile = lists.tile(list(src.shape), U16, name=name)
            nc.sync.dma_start(tile[:], src)
            return tile

        wq_plane_raw = scale_plane("wq_plane_raw", K, nc.gpsimd)
        arch_plane = scale_plane("arch_plane", TOKENS)
        cache_plane = scale_plane("cache_plane", TOKENS)
        draft_plane = scale_plane("draft_plane", TOKENS)

        states_raw = sb.tile([P, PACK, Q], F32, name="states_raw")
        nc.sync.dma_start(states_raw[:], states.rearrange("(p j) q -> p j q", j=PACK))
        load_scales(wq_plane_raw, wq_scales)
        wq_raw = load_words("wq_raw", wq_words, 0, K)
        arch_codes = load_words("arch_codes", arch_words, 0, TOKENS)
        load_scales(arch_plane, arch_scales)
        cache_codes = load_words("cache_codes", cache_words, 0, TOKENS)
        load_scales(cache_plane, cache_scales)
        draft_codes = sb.tile([P, 2 * TOKENS], U8, name="draft_codes", align_bytes=64)
        nc.sync.dma_start(draft_codes[:].bitcast(I32), draft_words[0].bitcast(I32))
        load_scales(draft_plane, draft_scales)
        idx2 = load_list("idx2", offs2)
        idx = load_list("idx", offs)
        idx5 = load_list("idx5", offs5)
        idx4 = load_list("idx4", offs4)
        idx3 = load_list("idx3", offs3)
        idx8 = load_list("idx8", offs8)
        idx7 = load_list("idx7", offs7)
        idx6 = load_list("idx6", offs6)

        f3 = sb.tile([P, TOKENS], F32, name="f3")
        nc.vector.memset(f3[:], 0.0)

        states_bf = sb.tile([P, Q, PACK], BF16, name="states_bf", align_bytes=64)
        split = Q // 2
        nc.scalar.activation(
            states_bf[:, split:, :].rearrange("p (c i) t -> p c t i", i=4),
            states_raw[:, :, split:].rearrange("p t (c i) -> p c t i", i=4),
            COPY,
        )
        nc.vector.tensor_copy(
            states_bf[:, :split, :].rearrange("p (c i) t -> p c t i", i=4),
            states_raw[:, :, :split].rearrange("p t (c i) -> p c t i", i=4),
        )
        states_codes = sb.tile([P, Q], U32, name="states_codes", align_bytes=64)
        states_plane = sb.tile([P, Q], U8, name="states_plane", align_bytes=64)
        nc.vector.quantize_mx(
            states_codes[:].bitcast(FP8X4), states_plane[:], states_bf[:].rearrange("p q t -> p (q t)")
        )

        wq_plane = sb.tile([P, K], U8, name="wq_plane", align_bytes=64)
        nc.vector.tensor_copy(
            wq_plane[:].rearrange("p (t m) -> p t m", t=PACK),
            wq_plane_raw[:].rearrange("p (m t) -> p t m", t=PACK),
        )
        wq_by_place = wq_raw[:].rearrange("p (c i t) -> p c t i", t=PACK, i=4)
        wq_codes = []
        for first, count in ((0, 2), (2, 1), (3, 1)):
            part = sb.tile([P, count, P], U32, name="wq_codes%d" % first, align_bytes=64)
            dst = part[:].rearrange("p t (c i) -> p c t i", i=4)
            src = wq_by_place[:, :, first : first + count, :]
            if first < 3:
                nc.scalar.copy(dst, src)
            else:
                nc.vector.tensor_copy(dst.bitcast(I32), src.bitcast(I32))
            wq_codes.extend(part[:, t, :] for t in range(count))

        f2 = sb.tile([P, TOKENS], F32, name="f2", tag="wq_raw", align_bytes=64)
        nc.vector.memset(f2[:], 0.0)
        qv_ps = psum.tile([P, PACK, Q], F32, name="qv_ps", tag="b_ps768")
        for t in range(PACK):
            cols = slice(P * t, P * (t + 1))
            nc.tensor.matmul_mx(
                qv_ps[:, t, :],
                lhsT=wq_codes[t].bitcast(FP8X4), lhsT_scale=wq_plane[:, cols],
                rhs=states_codes[:].bitcast(FP8X4), rhs_scale=states_plane[:],
                start=True, stop=True,
            )
        def score(name, codes, plane, moving, moving_plane):
            bank = psum.tile([P, moving_plane.shape[1]], F32, name=name, tag=name)
            nc.tensor.matmul_mx(
                bank[:], lhsT=codes[:].bitcast(FP8X4), lhsT_scale=plane[:],
                rhs=moving, rhs_scale=moving_plane, start=True, stop=True,
            )
            return bank

        c_ps = [
            score("c_ps%d" % h, states_codes, states_plane,
                  arch_codes[:, BANK * h : BANK * (h + 1)].bitcast(FP8X4),
                  arch_plane[:, BANK * h : BANK * (h + 1)])
            for h in range(2)
        ]

        qv_bf = sb.tile([P, Q, PACK], BF16, name="qv_bf", tag="qv_bf", align_bytes=64)
        nc.scalar.activation(qv_bf[:], qv_ps[:].rearrange("p t q -> p q t"), COPY)
        qv_codes = sb.tile([P, Q], U32, name="qv_codes", align_bytes=64)
        qv_plane = sb.tile([P, Q], U8, name="qv_plane", align_bytes=64)
        nc.vector.quantize_mx(qv_codes[:].bitcast(FP8X4), qv_plane[:], qv_bf[:].rearrange("p q t -> p (q t)"))
        f1 = sb.tile([P, TOKENS], F32, name="f1", tag="qv_bf", align_bytes=64)
        nc.vector.memset(f1[:], 0.0)

        b_cuts = [(0, 512), (512, 768), (768, 1024)]
        a_ps = [
            score("a_ps%d" % lo, qv_codes, qv_plane, cache_codes[:, lo:hi].bitcast(FP8X4), cache_plane[:, lo:hi])
            for lo, hi in b_cuts
        ]
        b_ps = [
            score("b_ps%d" % lo, qv_codes, qv_plane, draft_codes[:, 2 * lo : 2 * hi].bitcast(FP4X4),
                  draft_plane[:, lo:hi])
            for lo, hi in b_cuts
        ]

        late = slice(HALF // 16, SLOTS // 16)
        early = slice(0, HALF // 16)

        a = sb.tile([P, TOKENS], F32, name="a")
        b = sb.tile([P, TOKENS], F32, name="b")
        nc.scalar.activation(a[:, :BANK], a_ps[0][:], COPY)
        nc.vector.tensor_copy(a[:, 512:768], a_ps[1][:])
        nc.vector.tensor_copy(a[:, 768:1024], a_ps[2][:])
        a_late = sb.tile([P, HALF], F32, name="a_late")
        a_early = sb.tile([P, HALF], F32, name="a_early")
        nc.scalar.activation(a_late[:], a[:].indirect(idx2[:, late]), COPY)
        nc.vector.tensor_copy(b[:, 0:512], b_ps[0][:])
        nc.vector.tensor_copy(b[:, 512:768], b_ps[1][:])
        nc.scalar.activation(b[:, 768:1024], b_ps[2][:], COPY)
        w_late = sb.tile([P, HALF], F32, name="w_late")
        acc = sb.tile([P, HALF], F32, name="acc")
        nc.vector.tensor_tensor(w_late[:], b[:].indirect(idx[:, late]), a_late[:], SUB)
        nc.scalar.activation(a_early[:], a[:].indirect(idx2[:, early]), COPY)
        nc.vector.tensor_tensor(acc[:], b[:].indirect(idx[:, early]), a_early[:], SUB)

        nc.scalar.activation(f3[:].indirect(idx5[:]), w_late[:, RUN:], COPY)
        nc.scalar.activation(f2[:].indirect(idx4[:]), w_late[:, :RUN], COPY)
        nc.scalar.activation(f1[:].indirect(idx3[:]), acc[:], COPY)

        bb = sb.tile([P, TOKENS], F32, name="bb")
        cc = sb.tile([P, TOKENS], F32, name="cc")
        nc.gpsimd.tensor_tensor(bb[:, 768:], b[:, 768:], f3[:, 768:], SUB)
        for bank, (lo, hi) in zip(b_ps, b_cuts[:2]):
            nc.vector.tensor_tensor(bb[:, lo:hi], bank[:], f3[:, lo:hi], SUB)
        for h in range(2):
            cols = slice(BANK * h, BANK * (h + 1))
            nc.vector.tensor_tensor(cc[:, cols], c_ps[h][:], f2[:, cols], SUB)
        bb_early = sb.tile([P, HALF], F32, name="bb_early")
        nc.vector.tensor_copy(bb_early[:], bb[:].indirect(idx8[:, early]))
        aa = sb.tile([P, TOKENS], F32, name="aa", tag="wq_raw", align_bytes=64)
        nc.gpsimd.tensor_tensor(aa[:, 768:], a[:, 768:], f1[:, 768:], ADD)
        for bank, (lo, hi) in zip(a_ps, b_cuts[:2]):
            nc.vector.tensor_tensor(aa[:, lo:hi], bank[:], f1[:, lo:hi], ADD)

        cc_early = sb.tile([P, HALF], F32, name="cc_early")
        cc_late = sb.tile([P, HALF], F32, name="cc_late")
        aa_late = sb.tile([P, HALF], F32, name="aa_late")
        bb_late = sb.tile([P, HALF], F32, name="bb_late", tag="qv_bf", align_bytes=64)
        nc.scalar.activation(cc_early[:], cc[:].indirect(idx7[:, early]), COPY)
        nc.scalar.activation(cc_late[:], cc[:].indirect(idx7[:, late]), COPY)
        nc.scalar.activation(aa_late[:], aa[:].indirect(idx6[:, late]), COPY)
        nc.scalar.activation(bb_late[:], bb[:].indirect(idx8[:, late]), COPY)

        cc_less = sb.tile([P, HALF], F32, name="cc_less")
        aa_less = sb.tile([P, HALF], F32, name="aa_less")
        v_late = sb.tile([P, HALF], F32, name="v_late")
        y_early = sb.tile([P, HALF], F32, name="y_early")
        y_late = sb.tile([P, HALF], F32, name="y_late")
        nc.vector.tensor_tensor(cc_less[:], cc_early[:], bb_early[:], SUB)
        nc.vector.tensor_tensor(aa_less[:], aa[:].indirect(idx6[:, early]), bb_early[:], SUB)
        nc.vector.tensor_tensor(v_late[:], aa_late[:], cc_late[:], MAX)
        nc.vector.tensor_tensor(y_early[:], aa_less[:], cc_less[:], MAX)
        nc.sync.dma_start(out[:, :HALF], y_early[:])
        nc.vector.tensor_tensor(y_late[:], v_late[:], bb_late[:], SUB)
        nc.sync.dma_start(out[:, HALF:], y_late[:])
